import numpy as np, ml_dtypes
CORES = [15,47,79,175,207]
N = 5
import mx_ref
NC, G = 128, 4
C = np.float32(0.023)
BF = ml_dtypes.bfloat16
def cut(t, i, w=512):
    return t[:, w * i:w * i + w]
def tile(rs):
    return np.stack(rs, axis=2).reshape(128, -1).astype(BF)
def layer(w, X):
    out = []
    for i in range(G):
        for t in range(len(X)):
            p = mx_ref.matmul(mx_ref.quantize(cut(w, len(X) * i + t)), X[t])
            z = p if t == 0 else z + p
        out.append(z)
    return out
def act(Z):
    return [np.maximum(z, 0) * C for z in Z]
def setup_inputs(rng):
    def f(*shape):
        return mx_ref.flush((rng.standard_normal(shape, dtype=np.float32) * np.exp2(rng.integers(-2, 3, shape[:-1] + (1,)))).astype(BF))
    return {"x": f(N, 128, 4 * NC), "w1": f(N, 128, G * 512), "w2": f(N, 128, 512)}
def setup_inputs_blocks(rng):
    d = setup_inputs(rng)
    for k in ("x", "w1", "w2"): d[k] = mx_ref.spread(d[k], rng, 2)
    return d
def setup_inputs_wide(rng):
    d = setup_inputs(rng)
    for k in ("x", "w1", "w2"): d[k] = mx_ref.flush((d[k].astype(np.float32) * np.exp2(rng.integers(-6, 7, (N, 1, 1))).astype(np.float32)).astype(BF))
    return d
def reference(x, w1, w2):
    X = [mx_ref.quantize(x[j]) for j in range(N)]
    y = np.zeros((N, 128, NC), np.float32)
    for c in range(N):
        for r in range(N):
            p = mx_ref.matmul(mx_ref.quantize(w2[r]), mx_ref.quantize(tile(act(layer(w1[r], [X[c]])))))
            y[c] = p if r == 0 else y[c] + p
    return {"y": y}

@@ -1,0 +1,135 @@
+from concourse.bass import DstId, RemoteDMATransfer
+from concourse.mybir import dt, AluOpType, ActivationFunctionType
+
+N = 5
+NC = 128
+COEF = 0.023
+
+SCRATCH = {
+    "xb": ("sbuf", [128, 4 * NC], "bfloat16"),
+    "w1b": ("sbuf", [128, 4 * 512], "bfloat16"),
+    "w2b": ("sbuf", [128, 512], "bfloat16"),
+    "w1q": ("sbuf", [128, 512], "float8_e4m3fn_x4"),
+    "w1s": ("sbuf", [128, 512], "uint8"),
+    "w2q": ("sbuf", [128, 128], "float8_e4m3fn_x4"),
+    "w2s": ("sbuf", [128, 128], "uint8"),
+    "xq": ("sbuf", [128, N * NC], "float8_e4m3fn_x4"),
+    "xs": ("sbuf", [128, N * NC], "uint8"),
+    "h": ("sbuf", [128, N * 4 * NC], "bfloat16"),
+    "hq": ("sbuf", [128, N * NC], "float8_e4m3fn_x4"),
+    "hs": ("sbuf", [128, N * NC], "uint8"),
+    "yo": ("sbuf", [128, N * NC], "float32"),
+    "yi": ("sbuf", [128, N * NC], "float32"),
+    "acc": ("sbuf", [128, N * NC], "float32"),
+    "pz": ("psum", [128, 4 * 512], "float32"),
+    "py": ("psum", [128, 4 * 512], "float32"),
+}
+SEMAPHORES = (["ldx", "ldw1", "ldw2", "qx", "qw1", "qw2", "sent", "stored"]
+              + ["%s%d" % (s, c) for s in ("x", "r", "hq", "y", "cp", "s", "a") for c in range(N)]
+              + ["z%d_%d" % (c, b) for c in range(N) for b in range(4)])
+
+
+def rank_program(g, core, T, topo):
+    me = T.rank_of(core)
+    if me is None:
+        return
+    S = T.sem
+    dests = [(me + k) % N for k in range(1, N)]
+    srcs = [(me - k) % N for k in range(1, N)]
+    order = [me] + srcs
+
+    def slot(buf, c, w=NC):
+        return T[buf][:, c * w:(c + 1) * w]
+
+    def engines(dst):
+        m = topo.mask(core, T.cores[dst])
+        return m, bin(m).count("1")
+
+    def heard(src, dst):
+        return bin(topo.mask(T.cores[src], T.cores[dst])).count("1")
+
+    g.sync.dma_start(T.xb[:], T.x[:]).then_inc(S.ldx, 16)
+    g.sync.dma_start(T.w1b[:], T.w1[:]).then_inc(S.ldw1, 16)
+    g.sync.dma_start(T.w2b[:], T.w2[:]).then_inc(S.ldw2, 16)
+
+    sent = 0
+    g.wait_ge(S.qx, 1)
+    ids = []
+    for d in dests:
+        rid, pid = topo.addr(T.cores[d], core)
+        ids.append(DstId(rid=rid, pnc=pid))
+    m = topo.mask(core, T.cores[dests[0]])
+    for d in dests:
+        m &= topo.mask(core, T.cores[d])
+    g.remote_dma_fused([RemoteDMATransfer(dst_ids=ids, dma_engine_mask=m, remote_sem=S["x%d" % me],
+                                          src=slot("xs", me), dsts=[slot("xs", me) for d in dests])], local_sem=S.sent)
+    sent += bin(m).count("1")
+    for d in dests:
+        rid, pid = topo.addr(T.cores[d], core)
+        m, n = engines(d)
+        v = slot("xq", me).bitcast(dt.uint8)
+        g.remote_dma(v, v, S["x%d" % me], S.sent, pid, rid, m)
+        sent += n
+    for c in srcs:
+        rid, pid = topo.addr(T.cores[c], core)
+        m, n = engines(c)
+        g.wait_ge(S["cp%d" % c], 1)
+        g.remote_dma(slot("yi", me), slot("yo", c), S["s%d" % me], S.sent, pid, rid, m)
+        sent += n
+    g.wait_ge(S.sent, sent)
+
+    bank = {me: 0}
+    for i, c in enumerate(srcs):
+        bank[c] = 1 + i % 3
+    for i, c in enumerate(order):
+        if c == me:
+            g.tensor.wait_ge(S.qx, 1)
+            g.tensor.wait_ge(S.qw1, 1)
+        else:
+            g.tensor.wait_ge(S["x%d" % c], 2 * heard(c, me))
+        for b in range(4):
+            g.tensor.matmul_mx(T.pz[:, 512 * b:512 * b + NC], T.w1q[:, 128 * b:128 * b + 128], T.w1s[:, 128 * b:128 * b + 128],
+                               slot("xq", c), slot("xs", c), True, True).then_inc(S["z%d_%d" % (c, b)], 1)
+        if c == me:
+            g.tensor.wait_ge(S.qw2, 1)
+        if i == 4:
+            g.tensor.wait_ge(S["cp%d" % order[1]], 1)
+        g.tensor.wait_ge(S["hq%d" % c], 1)
+        g.tensor.matmul_mx(T.py[:, 512 * bank[c]:512 * bank[c] + NC], T.w2q[:], T.w2s[:],
+                           slot("hq", c), slot("hs", c), True, True).then_inc(S["y%d" % c], 1)
+
+    for c in order:
+        for b in (1, 3):
+            g.scalar.wait_ge(S["z%d_%d" % (c, b)], 1)
+            g.scalar.activation(T.h[:, 512 * c + b:512 * (c + 1):4], T.pz[:, 512 * b:512 * b + NC],
+                                ActivationFunctionType.Relu, scale=COEF).then_inc(S["r%d" % c], 1)
+        if c != me:
+            g.scalar.wait_ge(S["y%d" % c], 1)
+            g.scalar.activation(slot("yo", c), T.py[:, 512 * bank[c]:512 * bank[c] + NC],
+                                ActivationFunctionType.Copy).then_inc(S["cp%d" % c], 1)
+
+    g.vector.wait_ge(S.ldx, 16)
+    g.vector.quantize_mx(slot("xq", me), slot("xs", me), T.xb[:]).then_inc(S.qx, 1)
+    g.vector.wait_ge(S.ldw1, 16)
+    g.vector.quantize_mx(T.w1q[:], T.w1s[:], T.w1b[:]).then_inc(S.qw1, 1)
+    g.vector.wait_ge(S.ldw2, 16)
+    g.vector.quantize_mx(T.w2q[:], T.w2s[:], T.w2b[:]).then_inc(S.qw2, 1)
+    for c in order:
+        for b in (0, 2):
+            g.vector.wait_ge(S["z%d_%d" % (c, b)], 1)
+            g.vector.tensor_scalar(T.h[:, 512 * c + b:512 * (c + 1):4], T.pz[:, 512 * b:512 * b + NC],
+                                   0.0, COEF, AluOpType.max, AluOpType.mult).then_inc(S["r%d" % c], 1)
+        g.vector.wait_ge(S["r%d" % c], 4)
+        g.vector.quantize_mx(slot("hq", c), slot("hs", c), slot("h", c, 4 * NC)).then_inc(S["hq%d" % c], 1)
+    g.vector.wait_ge(S["y%d" % me], 1)
+    prev = T.py[:, 0:NC]
+    for i, r in enumerate(dests):
+        g.vector.wait_ge(S["s%d" % r], heard(r, me))
+        if i:
+            g.vector.wait_ge(S["a%d" % (i - 1)], 1)
+        g.vector.tensor_tensor(slot("acc", i), prev, slot("yi", r), AluOpType.add).then_inc(S["a%d" % i], 1)
+        prev = slot("acc", i)
+
+    g.sync.wait_ge(S["a%d" % (N - 2)], 1)
+    g.sync.dma_start(T.y[:], prev).then_inc(S.stored, 16)
+    g.sync.wait_ge(S.stored, 16)

@@ -21,10 +21,10 @@ SCRATCH = {
     "yo": ("sbuf", [128, N * NC], "float32"),
     "yi": ("sbuf", [128, N * NC], "float32"),
     "acc": ("sbuf", [128, N * NC], "float32"),
-    "pz": ("psum", [128, 4 * 512], "float32"),
-    "py": ("psum", [128, 4 * 512], "float32"),
+    "pz0": ("psum", [128, 4 * 512], "float32"),
+    "pz1": ("psum", [128, 4 * 512], "float32"),
 }
-SEMAPHORES = (["ldx", "ldw1", "ldw2", "qx", "qw1", "qw2", "sent", "stored"]
+SEMAPHORES = (["ldx", "ldw1a", "ldw1b", "ldw2", "qx", "qw1a", "qw1b", "qw2", "sent", "stored"]
               + ["%s%d" % (s, c) for s in ("x", "r", "hq", "y", "cp", "s", "a") for c in range(N)]
               + ["z%d_%d" % (c, b) for c in range(N) for b in range(4)])
 
@@ -37,92 +37,114 @@ def rank_program(g, core, T, topo):
     dests = [(me + k) % N for k in range(1, N)]
     srcs = [(me - k) % N for k in range(1, N)]
     order = [me] + srcs
+    psum = {c: T["pz%d" % (i % 2)] for i, c in enumerate(order)}
 
     def slot(buf, c, w=NC):
         return T[buf][:, c * w:(c + 1) * w]
 
-    def engines(dst):
-        m = topo.mask(core, T.cores[dst])
-        return m, bin(m).count("1")
+    def bank(c, b):
+        return psum[c][:, 512 * b:512 * b + NC]
+
+    def bits(m):
+        return bin(m).count("1")
 
     def heard(src, dst):
-        return bin(topo.mask(T.cores[src], T.cores[dst])).count("1")
+        return bits(topo.mask(T.cores[src], T.cores[dst]))
 
     g.sync.dma_start(T.xb[:], T.x[:]).then_inc(S.ldx, 16)
-    g.sync.dma_start(T.w1b[:], T.w1[:]).then_inc(S.ldw1, 16)
+    g.sync.dma_start(T.w1b[:, 0:1024], T.w1[:, 0:1024]).then_inc(S.ldw1a, 16)
+    g.sync.dma_start(T.w1b[:, 1024:2048], T.w1[:, 1024:2048]).then_inc(S.ldw1b, 16)
     g.sync.dma_start(T.w2b[:], T.w2[:]).then_inc(S.ldw2, 16)
 
     sent = 0
-    g.wait_ge(S.qx, 1)
-    ids = []
-    for d in dests:
-        rid, pid = topo.addr(T.cores[d], core)
-        ids.append(DstId(rid=rid, pnc=pid))
     m = topo.mask(core, T.cores[dests[0]])
     for d in dests:
         m &= topo.mask(core, T.cores[d])
-    g.remote_dma_fused([RemoteDMATransfer(dst_ids=ids, dma_engine_mask=m, remote_sem=S["x%d" % me],
-                                          src=slot("xs", me), dsts=[slot("xs", me) for d in dests])], local_sem=S.sent)
-    sent += bin(m).count("1")
-    for d in dests:
-        rid, pid = topo.addr(T.cores[d], core)
-        m, n = engines(d)
-        v = slot("xq", me).bitcast(dt.uint8)
-        g.remote_dma(v, v, S["x%d" % me], S.sent, pid, rid, m)
-        sent += n
+    g.wait_ge(S.qx, 1)
+    plane = slot("xs", me)
+    codes = slot("xq", me).bitcast(dt.uint8)
+    for pair in (dests[:2], dests[2:]):
+        at = [topo.addr(T.cores[d], core) for d in pair]
+        g.remote_dma_fused([RemoteDMATransfer(dst_ids=[DstId(rid=rid, pnc=pid) for rid, pid in at], dma_engine_mask=m,
+                                              remote_sem=S["x%d" % me], src=plane, dsts=[plane for d in pair])],
+                           local_sem=S.sent)
+        for rid, pid in at:
+            g.remote_dma(codes, codes, S["x%d" % me], S.sent, pid, rid, m)
+        sent += 3 * bits(m)
     for c in srcs:
         rid, pid = topo.addr(T.cores[c], core)
-        m, n = engines(c)
+        m = topo.mask(core, T.cores[c])
         g.wait_ge(S["cp%d" % c], 1)
         g.remote_dma(slot("yi", me), slot("yo", c), S["s%d" % me], S.sent, pid, rid, m)
-        sent += n
+        sent += bits(m)
     g.wait_ge(S.sent, sent)
 
-    bank = {me: 0}
-    for i, c in enumerate(srcs):
-        bank[c] = 1 + i % 3
-    for i, c in enumerate(order):
-        if c == me:
+    def first(i):
+        c = order[i]
+        if i == 0:
             g.tensor.wait_ge(S.qx, 1)
-            g.tensor.wait_ge(S.qw1, 1)
         else:
             g.tensor.wait_ge(S["x%d" % c], 2 * heard(c, me))
         for b in range(4):
-            g.tensor.matmul_mx(T.pz[:, 512 * b:512 * b + NC], T.w1q[:, 128 * b:128 * b + 128], T.w1s[:, 128 * b:128 * b + 128],
+            if i == 0 and b in (0, 2):
+                g.tensor.wait_ge(S["qw1a" if b == 0 else "qw1b"], 1)
+            if i > 1 and b == 3:
+                g.tensor.wait_ge(S["cp%d" % order[i - 2]], 1)
+            g.tensor.matmul_mx(bank(c, b), T.w1q[:, 128 * b:128 * b + 128], T.w1s[:, 128 * b:128 * b + 128],
                                slot("xq", c), slot("xs", c), True, True).then_inc(S["z%d_%d" % (c, b)], 1)
-        if c == me:
-            g.tensor.wait_ge(S.qw2, 1)
-        if i == 4:
-            g.tensor.wait_ge(S["cp%d" % order[1]], 1)
-        g.tensor.wait_ge(S["hq%d" % c], 1)
-        g.tensor.matmul_mx(T.py[:, 512 * bank[c]:512 * bank[c] + NC], T.w2q[:], T.w2s[:],
-                           slot("hq", c), slot("hs", c), True, True).then_inc(S["y%d" % c], 1)
 
-    for c in order:
+    def second(i):
+        c = order[i]
+        if i == 0:
+            g.tensor.wait_ge(S.qw2, 1)
+        g.tensor.wait_ge(S["hq%d" % c], 1)
+        g.tensor.matmul_mx(bank(c, 3), T.w2q[:], T.w2s[:], slot("hq", c), slot("hs", c), True, True).then_inc(S["y%d" % c], 1)
+
+    first(0)
+    second(0)
+    first(1)
+    for i in range(2, N):
+        first(i)
+        second(i - 1)
+    second(N - 1)
+
+    def relu13(i):
+        c = order[i]
         for b in (1, 3):
             g.scalar.wait_ge(S["z%d_%d" % (c, b)], 1)
-            g.scalar.activation(T.h[:, 512 * c + b:512 * (c + 1):4], T.pz[:, 512 * b:512 * b + NC],
+            g.scalar.activation(T.h[:, 512 * c + b:512 * (c + 1):4], bank(c, b),
                                 ActivationFunctionType.Relu, scale=COEF).then_inc(S["r%d" % c], 1)
-        if c != me:
-            g.scalar.wait_ge(S["y%d" % c], 1)
-            g.scalar.activation(slot("yo", c), T.py[:, 512 * bank[c]:512 * bank[c] + NC],
-                                ActivationFunctionType.Copy).then_inc(S["cp%d" % c], 1)
+
+    def copy(i):
+        c = order[i]
+        g.scalar.wait_ge(S["y%d" % c], 1)
+        g.scalar.activation(slot("yo", c), bank(c, 3), ActivationFunctionType.Copy).then_inc(S["cp%d" % c], 1)
+
+    relu13(0)
+    copy(0)
+    relu13(1)
+    for i in range(2, N):
+        relu13(i)
+        copy(i - 1)
+    copy(N - 1)
 
     g.vector.wait_ge(S.ldx, 16)
     g.vector.quantize_mx(slot("xq", me), slot("xs", me), T.xb[:]).then_inc(S.qx, 1)
-    g.vector.wait_ge(S.ldw1, 16)
-    g.vector.quantize_mx(T.w1q[:], T.w1s[:], T.w1b[:]).then_inc(S.qw1, 1)
+    g.vector.wait_ge(S.ldw1a, 16)
+    g.vector.quantize_mx(T.w1q[:, 0:256], T.w1s[:, 0:256], T.w1b[:, 0:1024]).then_inc(S.qw1a, 1)
+    g.vector.wait_ge(S.ldw1b, 16)
+    g.vector.quantize_mx(T.w1q[:, 256:512], T.w1s[:, 256:512], T.w1b[:, 1024:2048]).then_inc(S.qw1b, 1)
     g.vector.wait_ge(S.ldw2, 16)
     g.vector.quantize_mx(T.w2q[:], T.w2s[:], T.w2b[:]).then_inc(S.qw2, 1)
     for c in order:
         for b in (0, 2):
             g.vector.wait_ge(S["z%d_%d" % (c, b)], 1)
-            g.vector.tensor_scalar(T.h[:, 512 * c + b:512 * (c + 1):4], T.pz[:, 512 * b:512 * b + NC],
+            g.vector.tensor_scalar(T.h[:, 512 * c + b:512 * (c + 1):4], bank(c, b),
                                    0.0, COEF, AluOpType.max, AluOpType.mult).then_inc(S["r%d" % c], 1)
         g.vector.wait_ge(S["r%d" % c], 4)
         g.vector.quantize_mx(slot("hq", c), slot("hs", c), slot("h", c, 4 * NC)).then_inc(S["hq%d" % c], 1)
-    g.vector.wait_ge(S["y%d" % me], 1)
-    prev = T.py[:, 0:NC]
+    g.vector.wait_ge(S["cp%d" % me], 1)
+    prev = slot("yo", me)
     for i, r in enumerate(dests):
         g.vector.wait_ge(S["s%d" % r], heard(r, me))
         if i:

from concourse.bass import DstId, RemoteDMATransfer
from concourse.mybir import dt, AluOpType, ActivationFunctionType

N = 5
NC = 128
COEF = 0.023

SCRATCH = {
    "xb": ("sbuf", [128, 4 * NC], "bfloat16"),
    "w1b": ("sbuf", [128, 4 * 512], "bfloat16"),
    "w2b": ("sbuf", [128, 512], "bfloat16"),
    "w1q": ("sbuf", [128, 512], "float8_e4m3fn_x4"),
    "w1s": ("sbuf", [128, 512], "uint8"),
    "w2q": ("sbuf", [128, 128], "float8_e4m3fn_x4"),
    "w2s": ("sbuf", [128, 128], "uint8"),
    "xq": ("sbuf", [128, N * NC], "float8_e4m3fn_x4"),
    "xs": ("sbuf", [128, N * NC], "uint8"),
    "h": ("sbuf", [128, N * 4 * NC], "bfloat16"),
    "hq": ("sbuf", [128, N * NC], "float8_e4m3fn_x4"),
    "hs": ("sbuf", [128, N * NC], "uint8"),
    "yo": ("sbuf", [128, N * NC], "float32"),
    "yi": ("sbuf", [128, N * NC], "float32"),
    "acc": ("sbuf", [128, N * NC], "float32"),
    "pz0": ("psum", [128, 4 * 512], "float32"),
    "pz1": ("psum", [128, 4 * 512], "float32"),
}
SEMAPHORES = (["ldx", "ldw1a", "ldw1b", "ldw2", "qx", "qw1a", "qw1b", "qw2", "sent", "stored"]
              + ["%s%d" % (s, c) for s in ("x", "r", "hq", "y", "cp", "s", "a") for c in range(N)]
              + ["z%d_%d" % (c, b) for c in range(N) for b in range(4)])


def rank_program(g, core, T, topo):
    me = T.rank_of(core)
    if me is None:
        return
    S = T.sem
    dests = [(me + k) % N for k in range(1, N)]
    srcs = [(me - k) % N for k in range(1, N)]
    order = [me] + srcs
    psum = {c: T["pz%d" % (i % 2)] for i, c in enumerate(order)}

    def slot(buf, c, w=NC):
        return T[buf][:, c * w:(c + 1) * w]

    def bank(c, b):
        return psum[c][:, 512 * b:512 * b + NC]

    def bits(m):
        return bin(m).count("1")

    def heard(src, dst):
        return bits(topo.mask(T.cores[src], T.cores[dst]))

    g.sync.dma_start(T.xb[:], T.x[:]).then_inc(S.ldx, 16)
    g.sync.dma_start(T.w1b[:, 0:1024], T.w1[:, 0:1024]).then_inc(S.ldw1a, 16)
    g.sync.dma_start(T.w1b[:, 1024:2048], T.w1[:, 1024:2048]).then_inc(S.ldw1b, 16)
    g.sync.dma_start(T.w2b[:], T.w2[:]).then_inc(S.ldw2, 16)

    sent = 0
    m = topo.mask(core, T.cores[dests[0]])
    for d in dests:
        m &= topo.mask(core, T.cores[d])
    g.wait_ge(S.qx, 1)
    plane = slot("xs", me)
    codes = slot("xq", me).bitcast(dt.uint8)
    for pair in (dests[:2], dests[2:]):
        at = [topo.addr(T.cores[d], core) for d in pair]
        g.remote_dma_fused([RemoteDMATransfer(dst_ids=[DstId(rid=rid, pnc=pid) for rid, pid in at], dma_engine_mask=m,
                                              remote_sem=S["x%d" % me], src=plane, dsts=[plane for d in pair])],
                           local_sem=S.sent)
        for rid, pid in at:
            g.remote_dma(codes, codes, S["x%d" % me], S.sent, pid, rid, m)
        sent += 3 * bits(m)
    for c in srcs:
        rid, pid = topo.addr(T.cores[c], core)
        m = topo.mask(core, T.cores[c])
        g.wait_ge(S["cp%d" % c], 1)
        g.remote_dma(slot("yi", me), slot("yo", c), S["s%d" % me], S.sent, pid, rid, m)
        sent += bits(m)
    g.wait_ge(S.sent, sent)

    def first(i):
        c = order[i]
        if i == 0:
            g.tensor.wait_ge(S.qx, 1)
        else:
            g.tensor.wait_ge(S["x%d" % c], 2 * heard(c, me))
        for b in range(4):
            if i == 0 and b in (0, 2):
                g.tensor.wait_ge(S["qw1a" if b == 0 else "qw1b"], 1)
            if i > 1 and b == 3:
                g.tensor.wait_ge(S["cp%d" % order[i - 2]], 1)
            g.tensor.matmul_mx(bank(c, b), T.w1q[:, 128 * b:128 * b + 128], T.w1s[:, 128 * b:128 * b + 128],
                               slot("xq", c), slot("xs", c), True, True).then_inc(S["z%d_%d" % (c, b)], 1)

    def second(i):
        c = order[i]
        if i == 0:
            g.tensor.wait_ge(S.qw2, 1)
        g.tensor.wait_ge(S["hq%d" % c], 1)
        g.tensor.matmul_mx(bank(c, 3), T.w2q[:], T.w2s[:], slot("hq", c), slot("hs", c), True, True).then_inc(S["y%d" % c], 1)

    first(0)
    second(0)
    first(1)
    for i in range(2, N):
        first(i)
        second(i - 1)
    second(N - 1)

    def relu13(i):
        c = order[i]
        for b in (1, 3):
            g.scalar.wait_ge(S["z%d_%d" % (c, b)], 1)
            g.scalar.activation(T.h[:, 512 * c + b:512 * (c + 1):4], bank(c, b),
                                ActivationFunctionType.Relu, scale=COEF).then_inc(S["r%d" % c], 1)

    def copy(i):
        c = order[i]
        g.scalar.wait_ge(S["y%d" % c], 1)
        g.scalar.activation(slot("yo", c), bank(c, 3), ActivationFunctionType.Copy).then_inc(S["cp%d" % c], 1)

    relu13(0)
    copy(0)
    relu13(1)
    for i in range(2, N):
        relu13(i)
        copy(i - 1)
    copy(N - 1)

    g.vector.wait_ge(S.ldx, 16)
    g.vector.quantize_mx(slot("xq", me), slot("xs", me), T.xb[:]).then_inc(S.qx, 1)
    g.vector.wait_ge(S.ldw1a, 16)
    g.vector.quantize_mx(T.w1q[:, 0:256], T.w1s[:, 0:256], T.w1b[:, 0:1024]).then_inc(S.qw1a, 1)
    g.vector.wait_ge(S.ldw1b, 16)
    g.vector.quantize_mx(T.w1q[:, 256:512], T.w1s[:, 256:512], T.w1b[:, 1024:2048]).then_inc(S.qw1b, 1)
    g.vector.wait_ge(S.ldw2, 16)
    g.vector.quantize_mx(T.w2q[:], T.w2s[:], T.w2b[:]).then_inc(S.qw2, 1)
    for c in order:
        for b in (0, 2):
            g.vector.wait_ge(S["z%d_%d" % (c, b)], 1)
            g.vector.tensor_scalar(T.h[:, 512 * c + b:512 * (c + 1):4], bank(c, b),
                                   0.0, COEF, AluOpType.max, AluOpType.mult).then_inc(S["r%d" % c], 1)
        g.vector.wait_ge(S["r%d" % c], 4)
        g.vector.quantize_mx(slot("hq", c), slot("hs", c), slot("h", c, 4 * NC)).then_inc(S["hq%d" % c], 1)
    g.vector.wait_ge(S["cp%d" % me], 1)
    prev = slot("yo", me)
    for i, r in enumerate(dests):
        g.vector.wait_ge(S["s%d" % r], heard(r, me))
        if i:
            g.vector.wait_ge(S["a%d" % (i - 1)], 1)
        g.vector.tensor_tensor(slot("acc", i), prev, slot("yi", r), AluOpType.add).then_inc(S["a%d" % i], 1)
        prev = slot("acc", i)

    g.sync.wait_ge(S["a%d" % (N - 2)], 1)
    g.sync.dma_start(T.y[:], prev).then_inc(S.stored, 16)
    g.sync.wait_ge(S.stored, 16)
